import numpy as np, ml_dtypes
CORES = [242,247,114,119]
N = 4
TK = 128
def silu(z): return z / (1.0 + np.exp(-z))
def setup_inputs(rng):
    return {"x": rng.standard_normal((N, 128, TK), dtype=np.float32).astype(ml_dtypes.bfloat16), "w1": (rng.standard_normal((N, 128, 128), dtype=np.float32) / 8).astype(ml_dtypes.bfloat16), "w3": (rng.standard_normal((N, 128, 128), dtype=np.float32) / 8).astype(ml_dtypes.bfloat16), "w2": (rng.standard_normal((N, 128, 128), dtype=np.float32) / 8).astype(ml_dtypes.bfloat16)}
def setup_inputs_big(rng):
    d = setup_inputs(rng)
    for k in ("x",): d[k] = (d[k].astype(np.float32) * 1024.0).astype(d[k].dtype)
    return d
def setup_inputs_small(rng):
    d = setup_inputs(rng)
    for k in ("x",): d[k] = (d[k].astype(np.float32) * (1 / 1024.0)).astype(d[k].dtype)
    return d
def setup_inputs_apart(rng):
    d = setup_inputs(rng)
    f = (10.0 ** rng.permutation(np.linspace(-1.5, 1.5, N))).astype(np.float32).reshape(N, 1, 1)
    for k in ("x",): d[k] = (d[k].astype(np.float32) * f).astype(d[k].dtype)
    return d
def reference(x, w1, w3, w2):
    X, W1, W3, W2 = x.astype(np.float64), w1.astype(np.float64), w3.astype(np.float64), w2.astype(np.float64)
    y = np.zeros((N, 128, TK))
    for r in range(N):
        for j in range(N):
            y[r] += W2[j].T @ (silu(W1[j].T @ X[r]) * (W3[j].T @ X[r]))
    return {"y": y.astype(ml_dtypes.bfloat16)}

@@ -1,0 +1,115 @@
+from concourse.bass import DstId, RemoteDMATransfer
+from concourse.mybir import AluOpType, ActivationFunctionType
+
+D = 128
+WW = 3 * D
+NR = 4
+
+SCRATCH = {
+    "xs": ("sbuf", [128, D], "bfloat16"),
+    "w": ("sbuf", [128, NR * WW], "bfloat16"),
+    "s": ("sbuf", [128, NR * D], "float32"),
+    "h": ("sbuf", [128, NR * D], "bfloat16"),
+    "yo": ("sbuf", [128, D], "bfloat16"),
+    "p0": ("psum", [128, 512], "float32"),
+    "pa1": ("psum", [128, 512], "float32"), "pb1": ("psum", [128, 512], "float32"),
+    "pa2": ("psum", [128, 512], "float32"), "pb2": ("psum", [128, 512], "float32"),
+    "pa3": ("psum", [128, 512], "float32"), "pb3": ("psum", [128, 512], "float32"),
+    "py": ("psum", [128, 512], "float32"),
+}
+SEMAPHORES = (["wl", "xl", "sent", "yd", "yc", "st"] + ["arr%d" % j for j in range(NR)]
+              + ["%s%d" % (n, k) for n in ("za", "zb", "ac", "hh") for k in range(NR)])
+
+
+def _bits(m):
+    return [b for b in range(m.bit_length()) if (m >> b) & 1]
+
+
+def _on_chip(topo, a, b):
+    return topo.host(a) == topo.host(b) and topo.chip(a) == topo.chip(b)
+
+
+def _plan(topo, cores, src):
+    near = [c for c in cores if c != src and _on_chip(topo, src, c)]
+    far = [c for c in cores if c != src and not _on_chip(topo, src, c)]
+    leave = topo.mask(src, src)
+    for c in far:
+        leave &= topo.mask(src, c)
+    lb = _bits(leave)
+    per = len(lb) // len(far)
+    plan = {}
+    for i, c in enumerate(far):
+        plan[c] = sum(1 << b for b in lb[i * per:(i + 1) * per])
+    for c in near:
+        stay = _bits(topo.mask(src, c) & ~leave)
+        plan[c] = sum(1 << b for b in stay[::len(stay) // per])
+    return plan
+
+
+def rank_program(g, core, T, topo):
+    me = T.rank_of(core)
+    if me is None:
+        return
+    sem = T.sem
+    te, sc, ve, sy = g.tensor, g.scalar, g.vector, g.sync
+
+    def slot(j):
+        return T.w[:, j * WW:(j + 1) * WW]
+
+    def part(j, i):
+        return T.w[:, j * WW + i * D:j * WW + (i + 1) * D]
+
+    sy.dma_start(part(me, 0), T.w1[:]).then_inc(sem.wl, 16)
+    sc.dma_start(part(me, 1), T.w3[:]).then_inc(sem.wl, 16)
+    sy.dma_start(part(me, 2), T.w2[:]).then_inc(sem.wl, 16)
+    sc.dma_start(T.xs[:], T.x[:]).then_inc(sem.xl, 16)
+
+    plan = _plan(topo, T.cores, core)
+    trs, engines = [], 0
+    for c, m in plan.items():
+        rid, pid = topo.addr(c, core)
+        trs.append(RemoteDMATransfer(dst_ids=[DstId(rid=rid, pnc=pid)], dma_engine_mask=m,
+                                     remote_sem=sem["arr%d" % me], src=slot(me), dst=slot(me)))
+        engines += len(_bits(m))
+    g.wait_ge(sem.wl, 48)
+    g.remote_dma_fused(trs, local_sem=sem.sent)
+
+    others = [c for c in T.cores if c != core]
+    others.sort(key=lambda c: (not _on_chip(topo, core, c), topo.die(c) != topo.die(core)))
+    order = [core] + others
+    za = [T.p0[:, 0:D], T.pa1[:, 0:D], T.pa2[:, 0:D], T.pa3[:, 0:D]]
+    zb = [T.p0[:, D:2 * D], T.pb1[:, 0:D], T.pb2[:, 0:D], T.pb3[:, 0:D]]
+
+    def blk(t, k):
+        return t[:, k * D:(k + 1) * D]
+
+    def y_matmul(k):
+        te.wait_ge(sem["hh%d" % k], 1)
+        mm = te.matmul(T.py[:, 0:D], part(T.rank_of(order[k]), 2), blk(T.h, k), start=(k == 0), stop=(k == NR - 1))
+        if k == NR - 1:
+            mm.then_inc(sem.yd, 1)
+
+    te.wait_ge(sem.wl, 48)
+    te.wait_ge(sem.xl, 16)
+    for k, c in enumerate(order):
+        j = T.rank_of(c)
+        if k > 0:
+            te.wait_ge(sem["arr%d" % j], len(_bits(_plan(topo, T.cores, c)[core])))
+        te.matmul(za[k], part(j, 0), T.xs[:], start=True, stop=True).then_inc(sem["za%d" % k], 1)
+        te.matmul(zb[k], part(j, 1), T.xs[:], start=True, stop=True).then_inc(sem["za%d" % k if k == 0 else "zb%d" % k], 1)
+        if k > 0:
+            y_matmul(k - 1)
+        sc.wait_ge(sem["za%d" % k], 2 if k == 0 else 1)
+        sc.activation(blk(T.s, k), za[k], ActivationFunctionType.Silu).then_inc(sem["ac%d" % k], 1)
+        ve.wait_ge(sem["ac%d" % k], 1)
+        if k > 0:
+            ve.wait_ge(sem["zb%d" % k], 1)
+        ve.tensor_tensor(blk(T.h, k), blk(T.s, k), zb[k], AluOpType.mult).then_inc(sem["hh%d" % k], 1)
+    y_matmul(NR - 1)
+
+    ve.wait_ge(sem.yd, 1)
+    ve.tensor_copy(T.yo[:], T.py[:, 0:D]).then_inc(sem.yc, 1)
+    sy.wait_ge(sem.yc, 1)
+    sy.dma_start(T.y[:], T.yo[:]).then_inc(sem.st, 16)
+    sy.wait_ge(sem.st, 16)
+    g.wait_ge(sem.sent, engines)

@@ -4,6 +4,8 @@ from concourse.mybir import AluOpType, ActivationFunctionType
 D = 128
 WW = 3 * D
 NR = 4
+FAR_ENGINES = 4
+NEAR_ENGINES = 4
 
 SCRATCH = {
     "xs": ("sbuf", [128, D], "bfloat16"),
@@ -17,7 +19,7 @@ SCRATCH = {
     "pa3": ("psum", [128, 512], "float32"), "pb3": ("psum", [128, 512], "float32"),
     "py": ("psum", [128, 512], "float32"),
 }
-SEMAPHORES = (["wl", "xl", "sent", "yd", "yc", "st"] + ["arr%d" % j for j in range(NR)]
+SEMAPHORES = (["la", "lb", "xl", "sent", "yd", "yc", "st"] + ["%s%d" % (n, j) for n in ("aa", "ab") for j in range(NR)]
               + ["%s%d" % (n, k) for n in ("za", "zb", "ac", "hh") for k in range(NR)])
 
 
@@ -32,17 +34,17 @@ def _on_chip(topo, a, b):
 def _plan(topo, cores, src):
     near = [c for c in cores if c != src and _on_chip(topo, src, c)]
     far = [c for c in cores if c != src and not _on_chip(topo, src, c)]
-    leave = topo.mask(src, src)
+    leave = topo.mask(src, near[0])
     for c in far:
         leave &= topo.mask(src, c)
     lb = _bits(leave)
-    per = len(lb) // len(far)
+    lb = lb[::len(lb) // (FAR_ENGINES * len(far))]
     plan = {}
     for i, c in enumerate(far):
-        plan[c] = sum(1 << b for b in lb[i * per:(i + 1) * per])
+        plan[c] = sum(1 << b for b in lb[i * FAR_ENGINES:(i + 1) * FAR_ENGINES])
     for c in near:
         stay = _bits(topo.mask(src, c) & ~leave)
-        plan[c] = sum(1 << b for b in stay[::len(stay) // per])
+        plan[c] = sum(1 << b for b in stay[::len(stay) // NEAR_ENGINES])
     return plan
 
 
@@ -53,26 +55,25 @@ def rank_program(g, core, T, topo):
     sem = T.sem
     te, sc, ve, sy = g.tensor, g.scalar, g.vector, g.sync
 
-    def slot(j):
-        return T.w[:, j * WW:(j + 1) * WW]
+    def part(j, i, n=1):
+        return T.w[:, j * WW + i * D:j * WW + (i + n) * D]
 
-    def part(j, i):
-        return T.w[:, j * WW + i * D:j * WW + (i + 1) * D]
-
-    sy.dma_start(part(me, 0), T.w1[:]).then_inc(sem.wl, 16)
-    sc.dma_start(part(me, 1), T.w3[:]).then_inc(sem.wl, 16)
-    sy.dma_start(part(me, 2), T.w2[:]).then_inc(sem.wl, 16)
+    sy.dma_start(part(me, 0), T.w1[:]).then_inc(sem.la, 16)
+    sc.dma_start(part(me, 1), T.w3[:]).then_inc(sem.la, 16)
+    sy.dma_start(part(me, 2), T.w2[:]).then_inc(sem.lb, 16)
     sc.dma_start(T.xs[:], T.x[:]).then_inc(sem.xl, 16)
 
     plan = _plan(topo, T.cores, core)
-    trs, engines = [], 0
-    for c, m in plan.items():
-        rid, pid = topo.addr(c, core)
-        trs.append(RemoteDMATransfer(dst_ids=[DstId(rid=rid, pnc=pid)], dma_engine_mask=m,
-                                     remote_sem=sem["arr%d" % me], src=slot(me), dst=slot(me)))
-        engines += len(_bits(m))
-    g.wait_ge(sem.wl, 48)
-    g.remote_dma_fused(trs, local_sem=sem.sent)
+    engines = 0
+    for name, ap, loaded, n in (("aa", part(me, 0, 2), sem.la, 32), ("ab", part(me, 2), sem.lb, 16)):
+        trs = []
+        for c, m in plan.items():
+            rid, pid = topo.addr(c, core)
+            trs.append(RemoteDMATransfer(dst_ids=[DstId(rid=rid, pnc=pid)], dma_engine_mask=m,
+                                         remote_sem=sem["%s%d" % (name, me)], src=ap, dst=ap))
+            engines += len(_bits(m))
+        g.wait_ge(loaded, n)
+        g.remote_dma_fused(trs, local_sem=sem.sent)
 
     others = [c for c in T.cores if c != core]
     others.sort(key=lambda c: (not _on_chip(topo, core, c), topo.die(c) != topo.die(core)))
@@ -83,29 +84,37 @@ def rank_program(g, core, T, topo):
     def blk(t, k):
         return t[:, k * D:(k + 1) * D]
 
+    def count(c):
+        return len(_bits(_plan(topo, T.cores, c)[core]))
+
     def y_matmul(k):
+        if k == 0:
+            te.wait_ge(sem.lb, 16)
+        else:
+            te.wait_ge(sem["ab%d" % T.rank_of(order[k])], count(order[k]))
         te.wait_ge(sem["hh%d" % k], 1)
         mm = te.matmul(T.py[:, 0:D], part(T.rank_of(order[k]), 2), blk(T.h, k), start=(k == 0), stop=(k == NR - 1))
         if k == NR - 1:
             mm.then_inc(sem.yd, 1)
 
-    te.wait_ge(sem.wl, 48)
+    te.wait_ge(sem.la, 32)
     te.wait_ge(sem.xl, 16)
     for k, c in enumerate(order):
         j = T.rank_of(c)
         if k > 0:
-            te.wait_ge(sem["arr%d" % j], len(_bits(_plan(topo, T.cores, c)[core])))
+            te.wait_ge(sem["aa%d" % j], count(c))
         te.matmul(za[k], part(j, 0), T.xs[:], start=True, stop=True).then_inc(sem["za%d" % k], 1)
         te.matmul(zb[k], part(j, 1), T.xs[:], start=True, stop=True).then_inc(sem["za%d" % k if k == 0 else "zb%d" % k], 1)
-        if k > 0:
-            y_matmul(k - 1)
+        if k == 0:
+            y_matmul(0)
         sc.wait_ge(sem["za%d" % k], 2 if k == 0 else 1)
         sc.activation(blk(T.s, k), za[k], ActivationFunctionType.Silu).then_inc(sem["ac%d" % k], 1)
         ve.wait_ge(sem["ac%d" % k], 1)
         if k > 0:
             ve.wait_ge(sem["zb%d" % k], 1)
         ve.tensor_tensor(blk(T.h, k), blk(T.s, k), zb[k], AluOpType.mult).then_inc(sem["hh%d" % k], 1)
-    y_matmul(NR - 1)
+    for k in range(1, NR):
+        y_matmul(k)
 
     ve.wait_ge(sem.yd, 1)
     ve.tensor_copy(T.yo[:], T.py[:, 0:D]).then_inc(sem.yc, 1)

from concourse.bass import DstId, RemoteDMATransfer
from concourse.mybir import AluOpType, ActivationFunctionType

D = 128
WW = 3 * D
NR = 4
FAR_ENGINES = 4
NEAR_ENGINES = 4

SCRATCH = {
    "xs": ("sbuf", [128, D], "bfloat16"),
    "w": ("sbuf", [128, NR * WW], "bfloat16"),
    "s": ("sbuf", [128, NR * D], "float32"),
    "h": ("sbuf", [128, NR * D], "bfloat16"),
    "yo": ("sbuf", [128, D], "bfloat16"),
    "p0": ("psum", [128, 512], "float32"),
    "pa1": ("psum", [128, 512], "float32"), "pb1": ("psum", [128, 512], "float32"),
    "pa2": ("psum", [128, 512], "float32"), "pb2": ("psum", [128, 512], "float32"),
    "pa3": ("psum", [128, 512], "float32"), "pb3": ("psum", [128, 512], "float32"),
    "py": ("psum", [128, 512], "float32"),
}
SEMAPHORES = (["la", "lb", "xl", "sent", "yd", "yc", "st"] + ["%s%d" % (n, j) for n in ("aa", "ab") for j in range(NR)]
              + ["%s%d" % (n, k) for n in ("za", "zb", "ac", "hh") for k in range(NR)])


def _bits(m):
    return [b for b in range(m.bit_length()) if (m >> b) & 1]


def _on_chip(topo, a, b):
    return topo.host(a) == topo.host(b) and topo.chip(a) == topo.chip(b)


def _plan(topo, cores, src):
    near = [c for c in cores if c != src and _on_chip(topo, src, c)]
    far = [c for c in cores if c != src and not _on_chip(topo, src, c)]
    leave = topo.mask(src, near[0])
    for c in far:
        leave &= topo.mask(src, c)
    lb = _bits(leave)
    lb = lb[::len(lb) // (FAR_ENGINES * len(far))]
    plan = {}
    for i, c in enumerate(far):
        plan[c] = sum(1 << b for b in lb[i * FAR_ENGINES:(i + 1) * FAR_ENGINES])
    for c in near:
        stay = _bits(topo.mask(src, c) & ~leave)
        plan[c] = sum(1 << b for b in stay[::len(stay) // NEAR_ENGINES])
    return plan


def rank_program(g, core, T, topo):
    me = T.rank_of(core)
    if me is None:
        return
    sem = T.sem
    te, sc, ve, sy = g.tensor, g.scalar, g.vector, g.sync

    def part(j, i, n=1):
        return T.w[:, j * WW + i * D:j * WW + (i + n) * D]

    sy.dma_start(part(me, 0), T.w1[:]).then_inc(sem.la, 16)
    sc.dma_start(part(me, 1), T.w3[:]).then_inc(sem.la, 16)
    sy.dma_start(part(me, 2), T.w2[:]).then_inc(sem.lb, 16)
    sc.dma_start(T.xs[:], T.x[:]).then_inc(sem.xl, 16)

    plan = _plan(topo, T.cores, core)
    engines = 0
    for name, ap, loaded, n in (("aa", part(me, 0, 2), sem.la, 32), ("ab", part(me, 2), sem.lb, 16)):
        trs = []
        for c, m in plan.items():
            rid, pid = topo.addr(c, core)
            trs.append(RemoteDMATransfer(dst_ids=[DstId(rid=rid, pnc=pid)], dma_engine_mask=m,
                                         remote_sem=sem["%s%d" % (name, me)], src=ap, dst=ap))
            engines += len(_bits(m))
        g.wait_ge(loaded, n)
        g.remote_dma_fused(trs, local_sem=sem.sent)

    others = [c for c in T.cores if c != core]
    others.sort(key=lambda c: (not _on_chip(topo, core, c), topo.die(c) != topo.die(core)))
    order = [core] + others
    za = [T.p0[:, 0:D], T.pa1[:, 0:D], T.pa2[:, 0:D], T.pa3[:, 0:D]]
    zb = [T.p0[:, D:2 * D], T.pb1[:, 0:D], T.pb2[:, 0:D], T.pb3[:, 0:D]]

    def blk(t, k):
        return t[:, k * D:(k + 1) * D]

    def count(c):
        return len(_bits(_plan(topo, T.cores, c)[core]))

    def y_matmul(k):
        if k == 0:
            te.wait_ge(sem.lb, 16)
        else:
            te.wait_ge(sem["ab%d" % T.rank_of(order[k])], count(order[k]))
        te.wait_ge(sem["hh%d" % k], 1)
        mm = te.matmul(T.py[:, 0:D], part(T.rank_of(order[k]), 2), blk(T.h, k), start=(k == 0), stop=(k == NR - 1))
        if k == NR - 1:
            mm.then_inc(sem.yd, 1)

    te.wait_ge(sem.la, 32)
    te.wait_ge(sem.xl, 16)
    for k, c in enumerate(order):
        j = T.rank_of(c)
        if k > 0:
            te.wait_ge(sem["aa%d" % j], count(c))
        te.matmul(za[k], part(j, 0), T.xs[:], start=True, stop=True).then_inc(sem["za%d" % k], 1)
        te.matmul(zb[k], part(j, 1), T.xs[:], start=True, stop=True).then_inc(sem["za%d" % k if k == 0 else "zb%d" % k], 1)
        if k == 0:
            y_matmul(0)
        sc.wait_ge(sem["za%d" % k], 2 if k == 0 else 1)
        sc.activation(blk(T.s, k), za[k], ActivationFunctionType.Silu).then_inc(sem["ac%d" % k], 1)
        ve.wait_ge(sem["ac%d" % k], 1)
        if k > 0:
            ve.wait_ge(sem["zb%d" % k], 1)
        ve.tensor_tensor(blk(T.h, k), blk(T.s, k), zb[k], AluOpType.mult).then_inc(sem["hh%d" % k], 1)
    for k in range(1, NR):
        y_matmul(k)

    ve.wait_ge(sem.yd, 1)
    ve.tensor_copy(T.yo[:], T.py[:, 0:D]).then_inc(sem.yc, 1)
    sy.wait_ge(sem.yc, 1)
    sy.dma_start(T.y[:], T.yo[:]).then_inc(sem.st, 16)
    sy.wait_ge(sem.st, 16)
    g.wait_ge(sem.sent, engines)
